import numpy as np
import ml_dtypes


def mxq(x, axis, fmt="e4m3"):
    dtype, down = {"e4m3": (ml_dtypes.float8_e4m3fn, 7), "e5m2": (ml_dtypes.float8_e5m2, 14)}[fmt]
    v = np.moveaxis(np.asarray(x, np.float32).astype(ml_dtypes.bfloat16).astype(np.float64), axis, -1)
    blocks = v.reshape(v.shape[:-1] + (-1, 32))
    amax = np.abs(blocks).max(-1, keepdims=True)
    byte = np.maximum(np.where(amax > 0, np.frexp(amax)[1] - 1 + 127, 0) - down, 1)
    scale = np.exp2(byte - 127.0)
    codes = (blocks / scale).astype(np.float32).astype(dtype).astype(np.float64)
    return np.moveaxis((codes * scale).reshape(v.shape), -1, axis)


WIDE = False


def mx_kscale(k):
    if not WIDE:
        return np.ones(k)
    levels = np.array([10, -10, 5, -5, 0])
    if k % 512:
        return np.exp2(np.random.permutation(np.resize(levels, k // 32))).repeat(32)
    a = np.empty((k // 512, 16))
    for p in range(k // 512):
        a[p, :8] = np.random.permutation(np.resize(levels, 8))
        for g in range(8):
            far = levels[np.abs(levels - a[p, g]) >= 10]
            a[p, g + 8] = far[np.random.randint(len(far))]
    return np.exp2(a.ravel()).repeat(32)


def f64(x):
    return np.asarray(x).astype(np.float64)


def striped(idx):
    return np.tile(idx.reshape(-1, 16).T, (8, 1)).astype(np.uint16)


def unstriped(offs):
    return offs[:16].T.reshape(-1).astype(np.int64)


def striped8(idx):
    return np.concatenate([x.reshape(-1, 16).T for x in idx]).astype(np.uint16)


def runs(offs, k):
    lists = np.stack([offs[16 * r : 16 * r + 16].T.reshape(-1) for r in range(8)]).astype(np.int64)
    return lists[np.arange(k) % 512 // 64]


def pack_weight(w):
    k, n = w.shape
    w = f64(np.asarray(w, np.float32).astype(ml_dtypes.bfloat16)).reshape(k // 32, 32, n)
    amax = np.abs(w).max(1)
    byte = np.clip(np.where(amax > 0, np.frexp(amax)[1] - 1 + 127 - 7, 1), 1, 254)
    scaled = (w * np.exp2(127.0 - byte)[:, None, :]).reshape(k, n).astype(np.float32)
    words = np.ascontiguousarray(scaled.reshape(k // 512, 128, 4, n).transpose(0, 1, 3, 2)).astype(ml_dtypes.float8_e4m3fn).view(np.uint8)
    return words, np.ascontiguousarray(byte.astype(np.uint8).reshape(k // 512, 16, n))


def unpack_weight(words, scales):
    g, p, n, _ = words.shape
    vals = np.ascontiguousarray(words).view(ml_dtypes.float8_e4m3fn).astype(np.float64) * np.repeat(np.exp2(scales.astype(np.float64) - 127.0), 8, axis=1)[..., None]
    return vals.transpose(0, 1, 3, 2).reshape(g * 512, n)


K, T, S, H, C = 512, 2048, 512, 512, 512


def setup_inputs():
    n = np.random.standard_normal
    s = mx_kscale(K)[:, None]
    packed_xT = pack_weight(n((K, T)) * s)
    return {
        "x_words": packed_xT[0],
        "x_scales": packed_xT[1],
        "w1": (n((K, H)) / np.sqrt(K) / s).astype(np.float32),
        "gs": (np.random.uniform(0.5, 1.5, (K, 1)) / s).astype(np.float32),
        "offs": striped(np.random.permutation(T)[:S]),
        "n1": striped8(np.stack([np.random.permutation(S) for _ in range(8)])),
        "n2": striped8(np.stack([np.random.permutation(S) for _ in range(8)])),
        "ca": striped(np.random.permutation(T)[:C]),
        "cb": striped(np.random.permutation(T)[:C]),
        "n3": striped8(np.stack([np.random.permutation(S) for _ in range(8)])),
        "n4": striped8(np.stack([np.random.permutation(S) for _ in range(8)])),
    }


def reference(x_words, x_scales, w1, gs, offs, n1, n2, ca, cb, n3, n4):
    x_ca = unpack_weight(x_words, x_scales)[:, unstriped(ca)]
    xq = unpack_weight(x_words, x_scales)[:, unstriped(offs)]
    y = mxq(f64(w1), 0, "e4m3").T @ xq
    pa = y[np.arange(H)[:, None], runs(n1, H)]
    pb = y[np.arange(H)[:, None], runs(n2, H)]
    z = f64(gs) * (np.maximum(np.minimum(y, pa), np.minimum(np.maximum(y, pa), pb)))
    zq = mxq(z, 0, "e4m3")
    a = 0.0625 * (x_ca.T @ zq)
    x_cb = unpack_weight(x_words, x_scales)[:, unstriped(cb)]
    b = 0.0625 * (x_cb.T @ zq)
    return 0.75 * (a * (b[np.arange(C)[:, None], runs(n4, C)]) - ((a[np.arange(C)[:, None], runs(n3, C)]) * b))

@@ -1,0 +1,209 @@
+from contextlib import ExitStack
+
+import concourse.mybir as mybir
+
+K, T, S = 512, 2048, 512
+FLOPS = 3 * 2 * K * S * S
+
+F32 = mybir.dt.float32
+BF16 = mybir.dt.bfloat16
+I32 = mybir.dt.int32
+U32 = mybir.dt.uint32
+U16 = mybir.dt.uint16
+U8 = mybir.dt.uint8
+FP8X4 = mybir.dt.float8_e4m3fn_x4
+ALU = mybir.AluOpType
+COPY = mybir.ActivationFunctionType.Copy
+
+P = 128
+PACK = 4
+LIST_COLS = S // 16
+CHUNKS = ((0, 256), (256, 128), (384, 128))
+HALF = S // 2
+OUT_SCALE = 0.75 * 0.0625 * 0.0625
+
+
+def entries(offsets, start, width):
+    return offsets[:, start // 16 : (start + width) // 16]
+
+
+def tile_picked_ccmpcrossbmed_none_p_kernel(
+    tc, x_words, x_scales, w1, gs, offs, n1, n2, ca, cb, n3, n4, out
+):
+    nc = tc.nc
+    with ExitStack() as ctx:
+        lists = ctx.enter_context(tc.tile_pool(name="lists", bufs=1))
+        keep = ctx.enter_context(tc.tile_pool(name="keep", bufs=1))
+        psum = ctx.enter_context(tc.psum_pool(name="psum", bufs=1))
+
+        def load_list(name, src):
+            dst = lists.tile([P, LIST_COLS], U16, name=name)
+            nc.sync.dma_start(dst[:], src)
+            return dst
+
+        scale_table = keep.tile([P, T], U8, name="scale_table")
+        nc.vector.memset(scale_table[:].bitcast(I32), 0)
+        for q in range(4):
+            nc.scalar.dma_start(
+                scale_table[32 * q : 32 * q + 4, :].bitcast(I32),
+                x_scales[0, 4 * q : 4 * q + 4, :].bitcast(I32),
+            )
+        offs_l = load_list("offs_l", offs)
+        word_table = keep.tile([P, T], U32, name="word_table")
+        ca_l = load_list("ca_l", ca)
+        cb_l = load_list("cb_l", cb)
+        nc.sync.dma_start(word_table[:].bitcast(I32), x_words[0].rearrange("p c r -> p (c r)").bitcast(I32))
+        w_raw = keep.tile([P, PACK, S], F32, name="w_raw")
+        nc.sync.dma_start(w_raw[:], w1.rearrange("(p j) c -> p j c", j=PACK))
+        gain = keep.tile([P, PACK], F32, name="gain")
+        nc.gpsimd.dma_start(gain[:], gs.rearrange("(p t) o -> p (t o)", t=PACK))
+        n1_l = load_list("n1_l", n1)
+        n2_l = load_list("n2_l", n2)
+        n4_l = load_list("n4_l", n4)
+        n3_l = load_list("n3_l", n3)
+
+        x_sc = keep.tile([P, S], U8, name="x_sc", align_bytes=64)
+        nc.vector.tensor_copy(x_sc[:], scale_table[:].indirect(offs_l[:]))
+        pair_sc = []
+        for name, lst in (("a", ca_l), ("b", cb_l)):
+            picked = keep.tile([P, S], U8, name=name + "_sc_picked")
+            nc.vector.tensor_copy(picked[:], scale_table[:].indirect(lst[:]))
+            dealt = keep.tile([P, S], U8, name=name + "_sc", align_bytes=64)
+            nc.vector.tensor_copy(
+                dealt[:].rearrange("q (t m) -> q t m", t=PACK), picked[:].rearrange("q (m t) -> q t m", t=PACK)
+            )
+            pair_sc.append(dealt)
+        x_w = keep.tile([P, S], U32, name="x_w", align_bytes=64)
+        nc.vector.tensor_copy(x_w[:], word_table[:].indirect(offs_l[:]))
+
+        w_bf = keep.tile([P, PACK * S], BF16, name="w_bf", tag="w_then_a", align_bytes=64)
+        w_q = keep.tile([P, S], U32, name="w_q", align_bytes=64)
+        w_sc = keep.tile([P, S], U8, name="w_sc", align_bytes=64)
+        w_bf_v = w_bf[:].rearrange("p (t m j) -> p m j t", t=PACK, j=PACK)
+        w_raw_v = w_raw[:].rearrange("p j (m t) -> p m j t", t=PACK)
+        for u in range(2):
+            nc.scalar.activation(w_bf_v[:, :, :, 2 * u : 2 * u + 2], w_raw_v[:, :, :, 2 * u : 2 * u + 2], COPY)
+            nc.vector.quantize_mx(
+                out=w_q[:, u * HALF : (u + 1) * HALF].bitcast(FP8X4),
+                scales=w_sc[:, u * HALF : (u + 1) * HALF],
+                in_=w_bf[:, u * 2 * S : (u + 1) * 2 * S],
+            )
+
+        def pick_dealt_words(name, lst, tag):
+            dealt = keep.tile([P, S], U32, name=name, tag=tag, align_bytes=64)
+            nc.vector.tensor_copy(dealt[:].rearrange("q (t m) -> q m t", t=PACK), word_table[:].indirect(lst[:]))
+            return dealt
+
+        a_w = pick_dealt_words("a_w", ca_l, "w_then_a")
+
+        y_f32 = []
+        y_bank = []
+        y_bf = keep.tile([P, PACK, S], BF16, name="y_bf")
+        for t in range(PACK):
+            bank = psum.tile([P, S], F32, name="y_bank%d" % t, tag="bank%d" % (PACK + t))
+            nc.tensor.matmul_mx(
+                out=bank[:],
+                lhsT=w_q[:, t * P : (t + 1) * P].bitcast(FP8X4),
+                lhsT_scale=w_sc[:, t * P : (t + 1) * P],
+                rhs=x_w[:].bitcast(FP8X4),
+                rhs_scale=x_sc[:],
+                start=True,
+                stop=True,
+            )
+            y_t = keep.tile([P, S], F32, name="y%d" % t)
+            nc.scalar.activation(y_t[:], bank[:], COPY, scale=gain[:, t : t + 1])
+            y_f32.append(y_t)
+            y_bank.append(bank)
+        for t in range(PACK):
+            nc.scalar.activation(y_bf[:, t, :], y_bank[t][:], COPY, scale=gain[:, t : t + 1])
+
+        a_sb = [keep.tile([P, S], F32, name="a%d" % t) for t in range(PACK)]
+        b_sb = [keep.tile([P, S], F32, name="b%d" % t) for t in range(PACK)]
+        z_q = []
+        z_sc = []
+
+        def score(dst, words, scales, t, c):
+            nc.tensor.matmul_mx(
+                out=dst,
+                lhsT=words[:, t * P : (t + 1) * P].bitcast(FP8X4),
+                lhsT_scale=scales[:, t * P : (t + 1) * P],
+                rhs=z_q[c][:].bitcast(FP8X4),
+                rhs_scale=z_sc[c][:],
+                start=True,
+                stop=True,
+            )
+
+        last = len(CHUNKS) - 1
+        late0, late_w = CHUNKS[last]
+        a_early = [psum.tile([P, late0], F32, name="a_early%d" % t, tag="bank%d" % t) for t in range(PACK)]
+        pa_tags = ("pa", "pa", "z_k0")
+        pb_tags = ("pb", "pb", "z_k1")
+        for c, (c0, w) in enumerate(CHUNKS):
+            pa = keep.tile([P, PACK, w], BF16, name="pa%d" % c, tag=pa_tags[c], align_bytes=64)
+            pb = keep.tile([P, PACK, w], BF16, name="pb%d" % c, tag=pb_tags[c], align_bytes=64)
+            for t in range(PACK):
+                nc.vector.tensor_copy(pa[:, t, :], y_f32[t][:].indirect(entries(n1_l, c0, w)))
+                if c == 0:
+                    nc.vector.tensor_copy(pb[:, t, :], y_f32[t][:].indirect(entries(n2_l, c0, w)))
+            if c > 0:
+                for t in range(PACK):
+                    nc.vector.tensor_copy(pb[:, t, :], y_f32[t][:].indirect(entries(n2_l, c0, w)))
+            y_c = y_bf[:, :, c0 : c0 + w]
+            hi = keep.tile([P, PACK, w], BF16, name="hi%d" % c)
+            lo = keep.tile([P, PACK, w], BF16, name="lo%d" % c)
+            mid = keep.tile([P, PACK, w], BF16, name="mid%d" % c, tag="mid%d" % c, align_bytes=64)
+            z = keep.tile([P, PACK, w], BF16, name="z%d" % c)
+            nc.vector.tensor_tensor(hi[:], y_c, pa[:], ALU.max)
+            nc.vector.tensor_tensor(lo[:], y_c, pa[:], ALU.min)
+            nc.vector.tensor_tensor(mid[:], hi[:], pb[:], ALU.min)
+            nc.vector.tensor_tensor(z[:], lo[:], mid[:], ALU.max)
+            z_k = keep.tile([P, w * PACK], BF16, name="z_k%d" % c, tag="z_k%d" % c, align_bytes=64)
+            nc.scalar.copy(
+                z_k[:].rearrange("p (c i t) -> p c t i", i=4, t=PACK), z[:].rearrange("p t (c i) -> p c t i", i=4)
+            )
+            if c == last:
+                b_w = pick_dealt_words("b_w", cb_l, "mid%d" % c)
+            z_q.append(keep.tile([P, w], U32, name="z_q%d" % c, align_bytes=64))
+            z_sc.append(keep.tile([P, w], U8, name="z_sc%d" % c, align_bytes=64))
+            nc.vector.quantize_mx(out=z_q[c][:].bitcast(FP8X4), scales=z_sc[c][:], in_=z_k[:])
+            if c < last:
+                for t in range(PACK):
+                    score(a_early[t][:, c0 : c0 + w], a_w, pair_sc[0], t, c)
+            if c == last - 1:
+                nc.scalar.activation(a_sb[0][:, :late0], a_early[0][:], COPY, scale=OUT_SCALE)
+
+        for t in range(PACK):
+            b_early = psum.tile([P, late0], F32, name="b_early%d" % t, tag="bank%d" % (PACK + t))
+            for c in range(last):
+                c0, w = CHUNKS[c]
+                score(b_early[:, c0 : c0 + w], b_w, pair_sc[1], t, c)
+            if t > 0:
+                nc.scalar.activation(a_sb[t][:, :late0], a_early[t][:], COPY, scale=OUT_SCALE)
+            nc.scalar.copy(b_sb[t][:, :late0], b_early[:])
+            ab_late = psum.tile([P, 2, late_w], F32, name="ab_late%d" % t, tag="bank%d" % t)
+            score(ab_late[:, 0, :], a_w, pair_sc[0], t, last)
+            score(ab_late[:, 1, :], b_w, pair_sc[1], t, last)
+            nc.scalar.activation(a_sb[t][:, late0:], ab_late[:, 0, :], COPY, scale=OUT_SCALE)
+            nc.scalar.copy(b_sb[t][:, late0:], ab_late[:, 1, :])
+
+        out_v = out.rearrange("(p t) n -> t p n", t=PACK)
+        for t in range(PACK):
+            left = keep.tile([P, S], F32, name="left%d" % t)
+            right = keep.tile([P, S], F32, name="right%d" % t)
+            res = keep.tile([P, S], F32, name="res%d" % t)
+            for h in range(2):
+                cols = slice(h * HALF, (h + 1) * HALF)
+                nc.vector.tensor_tensor(
+                    left[:, cols], b_sb[t][:].indirect(entries(n4_l, h * HALF, HALF)), a_sb[t][:, cols], ALU.mult
+                )
+                nc.vector.tensor_tensor(
+                    right[:, cols], a_sb[t][:].indirect(entries(n3_l, h * HALF, HALF)), b_sb[t][:, cols], ALU.mult
+                )
+            if t < PACK - 1:
+                nc.vector.tensor_tensor(res[:], left[:], right[:], ALU.subtract)
+                nc.sync.dma_start(out_v[t], res[:])
+            else:
+                for h in range(2):
+                    cols = slice(h * HALF, (h + 1) * HALF)
+                    nc.vector.tensor_tensor(res[:, cols], left[:, cols], right[:, cols], ALU.subtract)
+                    nc.sync.dma_start(out_v[t][:, cols], res[:, cols])

@@ -1,6 +1,7 @@
 from contextlib import ExitStack
 
 import concourse.mybir as mybir
+from concourse.masks import make_identity
 
 K, T, S = 512, 2048, 512
 FLOPS = 3 * 2 * K * S * S
@@ -44,23 +45,26 @@ def tile_picked_ccmpcrossbmed_none_p_kernel(
         scale_table = keep.tile([P, T], U8, name="scale_table")
         nc.vector.memset(scale_table[:].bitcast(I32), 0)
         for q in range(4):
-            nc.scalar.dma_start(
+            nc.sync.dma_start(
                 scale_table[32 * q : 32 * q + 4, :].bitcast(I32),
                 x_scales[0, 4 * q : 4 * q + 4, :].bitcast(I32),
             )
         offs_l = load_list("offs_l", offs)
-        word_table = keep.tile([P, T], U32, name="word_table")
         ca_l = load_list("ca_l", ca)
         cb_l = load_list("cb_l", cb)
-        nc.sync.dma_start(word_table[:].bitcast(I32), x_words[0].rearrange("p c r -> p (c r)").bitcast(I32))
         w_raw = keep.tile([P, PACK, S], F32, name="w_raw")
         nc.sync.dma_start(w_raw[:], w1.rearrange("(p j) c -> p j c", j=PACK))
+        word_table = keep.tile([P, T], U32, name="word_table")
+        nc.sync.dma_start(word_table[:].bitcast(I32), x_words[0].rearrange("p c r -> p (c r)").bitcast(I32))
         gain = keep.tile([P, PACK], F32, name="gain")
-        nc.gpsimd.dma_start(gain[:], gs.rearrange("(p t) o -> p (t o)", t=PACK))
+        nc.sync.dma_start(gain[:], gs.rearrange("(p t) o -> p (t o)", t=PACK))
         n1_l = load_list("n1_l", n1)
         n2_l = load_list("n2_l", n2)
-        n4_l = load_list("n4_l", n4)
         n3_l = load_list("n3_l", n3)
+        n4_l = load_list("n4_l", n4)
+        ident = keep.tile([P, P], F32, name="ident")
+        nc.vector.memset(ident[:], 0.0)
+        make_identity(nc, ident[:], nomemset=True)
 
         x_sc = keep.tile([P, S], U8, name="x_sc", align_bytes=64)
         nc.vector.tensor_copy(x_sc[:], scale_table[:].indirect(offs_l[:]))
@@ -70,31 +74,35 @@ def tile_picked_ccmpcrossbmed_none_p_kernel(
             nc.vector.tensor_copy(picked[:], scale_table[:].indirect(lst[:]))
             dealt = keep.tile([P, S], U8, name=name + "_sc", align_bytes=64)
             nc.vector.tensor_copy(
-                dealt[:].rearrange("q (t m) -> q t m", t=PACK), picked[:].rearrange("q (m t) -> q t m", t=PACK)
+                dealt[:].bitcast(I32).rearrange("q (t r i) -> q t r i", t=PACK, i=4),
+                picked[:].bitcast(I32).rearrange("q (r t i) -> q t r i", t=PACK, i=4),
             )
             pair_sc.append(dealt)
         x_w = keep.tile([P, S], U32, name="x_w", align_bytes=64)
         nc.vector.tensor_copy(x_w[:], word_table[:].indirect(offs_l[:]))
 
-        w_bf = keep.tile([P, PACK * S], BF16, name="w_bf", tag="w_then_a", align_bytes=64)
         w_q = keep.tile([P, S], U32, name="w_q", align_bytes=64)
         w_sc = keep.tile([P, S], U8, name="w_sc", align_bytes=64)
-        w_bf_v = w_bf[:].rearrange("p (t m j) -> p m j t", t=PACK, j=PACK)
         w_raw_v = w_raw[:].rearrange("p j (m t) -> p m j t", t=PACK)
         for u in range(2):
-            nc.scalar.activation(w_bf_v[:, :, :, 2 * u : 2 * u + 2], w_raw_v[:, :, :, 2 * u : 2 * u + 2], COPY)
+            w_bf = keep.tile([P, 2 * S], BF16, name="w_bf%d" % u, tag="w_bf%d" % u, align_bytes=64)
+            nc.scalar.activation(
+                w_bf[:].rearrange("p (t m j) -> p m j t", t=2, j=PACK), w_raw_v[:, :, :, 2 * u : 2 * u + 2], COPY
+            )
             nc.vector.quantize_mx(
                 out=w_q[:, u * HALF : (u + 1) * HALF].bitcast(FP8X4),
                 scales=w_sc[:, u * HALF : (u + 1) * HALF],
-                in_=w_bf[:, u * 2 * S : (u + 1) * 2 * S],
+                in_=w_bf[:],
             )
 
         def pick_dealt_words(name, lst, tag):
             dealt = keep.tile([P, S], U32, name=name, tag=tag, align_bytes=64)
-            nc.vector.tensor_copy(dealt[:].rearrange("q (t m) -> q m t", t=PACK), word_table[:].indirect(lst[:]))
+            nc.vector.tensor_copy(
+                dealt[:].rearrange("q (t r i) -> q r t i", t=PACK, i=16), word_table[:].indirect(lst[:])
+            )
             return dealt
 
-        a_w = pick_dealt_words("a_w", ca_l, "w_then_a")
+        a_w = pick_dealt_words("a_w", ca_l, "w_bf1")
 
         y_f32 = []
         y_bank = []
@@ -117,30 +125,37 @@ def tile_picked_ccmpcrossbmed_none_p_kernel(
         for t in range(PACK):
             nc.scalar.activation(y_bf[:, t, :], y_bank[t][:], COPY, scale=gain[:, t : t + 1])
 
-        a_sb = [keep.tile([P, S], F32, name="a%d" % t) for t in range(PACK)]
-        b_sb = [keep.tile([P, S], F32, name="b%d" % t) for t in range(PACK)]
-        z_q = []
-        z_sc = []
+        z_q = keep.tile([P, S], U32, name="z_q", align_bytes=64)
+        z_sc = keep.tile([P, S], U8, name="z_sc", align_bytes=64)
 
-        def score(dst, words, scales, t, c):
+        def score(dst, words, scales, t, c0, w):
             nc.tensor.matmul_mx(
                 out=dst,
                 lhsT=words[:, t * P : (t + 1) * P].bitcast(FP8X4),
                 lhsT_scale=scales[:, t * P : (t + 1) * P],
-                rhs=z_q[c][:].bitcast(FP8X4),
-                rhs_scale=z_sc[c][:],
+                rhs=z_q[:, c0 : c0 + w].bitcast(FP8X4),
+                rhs_scale=z_sc[:, c0 : c0 + w],
                 start=True,
                 stop=True,
             )
 
+        last_t = PACK - 1
+        a_pos = [keep.tile([P, S], F32, name="a_pos%d" % t) for t in range(PACK)]
+        a_win = [keep.tile([P, S], F32, name="a_neg%d" % t) for t in range(last_t)] + [a_pos[last_t]]
+        b_sb = [keep.tile([P, S], F32, name="b%d" % t) for t in range(PACK)]
+
+        def a_out(t, src, c0, c1):
+            nc.scalar.activation(a_pos[t][:, c0:c1], src, COPY, scale=OUT_SCALE)
+            if t < last_t:
+                nc.scalar.activation(a_win[t][:, c0:c1], src, COPY, scale=-OUT_SCALE)
+
         last = len(CHUNKS) - 1
         late0, late_w = CHUNKS[last]
-        a_early = [psum.tile([P, late0], F32, name="a_early%d" % t, tag="bank%d" % t) for t in range(PACK)]
-        pa_tags = ("pa", "pa", "z_k0")
-        pb_tags = ("pb", "pb", "z_k1")
+        a_early = psum.tile([P, late0], F32, name="a_early", tag="bank0")
+        first_w = CHUNKS[0][1]
         for c, (c0, w) in enumerate(CHUNKS):
-            pa = keep.tile([P, PACK, w], BF16, name="pa%d" % c, tag=pa_tags[c], align_bytes=64)
-            pb = keep.tile([P, PACK, w], BF16, name="pb%d" % c, tag=pb_tags[c], align_bytes=64)
+            pa = keep.tile([P, PACK, w], BF16, name="pa%d" % c, tag="pa")
+            pb = keep.tile([P, PACK, w], BF16, name="pb%d" % c, tag="pb")
             for t in range(PACK):
                 nc.vector.tensor_copy(pa[:, t, :], y_f32[t][:].indirect(entries(n1_l, c0, w)))
                 if c == 0:
@@ -149,9 +164,9 @@ def tile_picked_ccmpcrossbmed_none_p_kernel(
                 for t in range(PACK):
                     nc.vector.tensor_copy(pb[:, t, :], y_f32[t][:].indirect(entries(n2_l, c0, w)))
             y_c = y_bf[:, :, c0 : c0 + w]
-            hi = keep.tile([P, PACK, w], BF16, name="hi%d" % c)
+            hi = keep.tile([P, PACK, w], BF16, name="hi%d" % c, tag="hi%d" % c, align_bytes=64)
             lo = keep.tile([P, PACK, w], BF16, name="lo%d" % c)
-            mid = keep.tile([P, PACK, w], BF16, name="mid%d" % c, tag="mid%d" % c, align_bytes=64)
+            mid = keep.tile([P, PACK, w], BF16, name="mid%d" % c)
             z = keep.tile([P, PACK, w], BF16, name="z%d" % c)
             nc.vector.tensor_tensor(hi[:], y_c, pa[:], ALU.max)
             nc.vector.tensor_tensor(lo[:], y_c, pa[:], ALU.min)
@@ -162,31 +177,39 @@ def tile_picked_ccmpcrossbmed_none_p_kernel(
                 z_k[:].rearrange("p (c i t) -> p c t i", i=4, t=PACK), z[:].rearrange("p t (c i) -> p c t i", i=4)
             )
             if c == last:
-                b_w = pick_dealt_words("b_w", cb_l, "mid%d" % c)
-            z_q.append(keep.tile([P, w], U32, name="z_q%d" % c, align_bytes=64))
-            z_sc.append(keep.tile([P, w], U8, name="z_sc%d" % c, align_bytes=64))
-            nc.vector.quantize_mx(out=z_q[c][:].bitcast(FP8X4), scales=z_sc[c][:], in_=z_k[:])
+                b_w = pick_dealt_words("b_w", cb_l, "hi%d" % c)
+            nc.vector.quantize_mx(
+                out=z_q[:, c0 : c0 + w].bitcast(FP8X4), scales=z_sc[:, c0 : c0 + w], in_=z_k[:]
+            )
             if c < last:
-                for t in range(PACK):
-                    score(a_early[t][:, c0 : c0 + w], a_w, pair_sc[0], t, c)
+                score(a_early[:, c0 : c0 + w], a_w, pair_sc[0], 0, c0, w)
+            if c == 0:
+                for t in range(1, PACK):
+                    a_first = psum.tile([P, first_w], F32, name="a_first%d" % t, tag="bank%d" % t)
+                    score(a_first[:], a_w, pair_sc[0], t, 0, first_w)
+                    a_out(t, a_first[:], 0, first_w)
             if c == last - 1:
-                nc.scalar.activation(a_sb[0][:, :late0], a_early[0][:], COPY, scale=OUT_SCALE)
+                a_out(0, a_early[:], 0, late0)
 
-        for t in range(PACK):
-            b_early = psum.tile([P, late0], F32, name="b_early%d" % t, tag="bank%d" % (PACK + t))
-            for c in range(last):
-                c0, w = CHUNKS[c]
-                score(b_early[:, c0 : c0 + w], b_w, pair_sc[1], t, c)
-            if t > 0:
-                nc.scalar.activation(a_sb[t][:, :late0], a_early[t][:], COPY, scale=OUT_SCALE)
-            nc.scalar.copy(b_sb[t][:, :late0], b_early[:])
-            ab_late = psum.tile([P, 2, late_w], F32, name="ab_late%d" % t, tag="bank%d" % t)
-            score(ab_late[:, 0, :], a_w, pair_sc[0], t, last)
-            score(ab_late[:, 1, :], b_w, pair_sc[1], t, last)
-            nc.scalar.activation(a_sb[t][:, late0:], ab_late[:, 0, :], COPY, scale=OUT_SCALE)
-            nc.scalar.copy(b_sb[t][:, late0:], ab_late[:, 1, :])
+        b_first = psum.tile([P, first_w], F32, name="b_first", tag="bank%d" % PACK)
+        score(b_first[:], b_w, pair_sc[1], 0, 0, first_w)
+        a_late = psum.tile([P, late_w], F32, name="a_late", tag="bank0")
+        score(a_late[:], a_w, pair_sc[0], 0, late0, late_w)
+        b_rest = psum.tile([P, S - first_w], F32, name="b_rest", tag="bank%d" % (2 * PACK - 1))
+        score(b_rest[:], b_w, pair_sc[1], 0, first_w, S - first_w)
+        nc.scalar.copy(b_sb[0][:, :first_w], b_first[:])
+        nc.scalar.activation(a_win[0][:, late0:], a_late[:], COPY, scale=-OUT_SCALE)
+        nc.scalar.copy(b_sb[0][:, first_w:], b_rest[:])
+        nc.scalar.activation(a_pos[0][:, late0:], a_late[:], COPY, scale=OUT_SCALE)
+        for t in range(1, PACK):
+            b_bank = psum.tile([P, S], F32, name="b_bank%d" % t, tag="bank%d" % (PACK + t))
+            score(b_bank[:], b_w, pair_sc[1], t, 0, S)
+            a_rest = psum.tile([P, S - first_w], F32, name="a_rest%d" % t, tag="bank%d" % t)
+            score(a_rest[:], a_w, pair_sc[0], t, first_w, S - first_w)
+            nc.scalar.copy(b_sb[t][:], b_bank[:])
+            a_out(t, a_rest[:], first_w, S)
 
-        out_v = out.rearrange("(p t) n -> t p n", t=PACK)
+        out_v = out.rearrange("(r t i) n -> t r i n", t=PACK, i=16)
         for t in range(PACK):
             left = keep.tile([P, S], F32, name="left%d" % t)
             right = keep.tile([P, S], F32, name="right%d" % t)
@@ -194,16 +217,28 @@ def tile_picked_ccmpcrossbmed_none_p_kernel(
             for h in range(2):
                 cols = slice(h * HALF, (h + 1) * HALF)
                 nc.vector.tensor_tensor(
-                    left[:, cols], b_sb[t][:].indirect(entries(n4_l, h * HALF, HALF)), a_sb[t][:, cols], ALU.mult
+                    right[:, cols], a_win[t][:].indirect(entries(n3_l, h * HALF, HALF)), b_sb[t][:, cols], ALU.mult
                 )
                 nc.vector.tensor_tensor(
-                    right[:, cols], a_sb[t][:].indirect(entries(n3_l, h * HALF, HALF)), b_sb[t][:, cols], ALU.mult
+                    left[:, cols], b_sb[t][:].indirect(entries(n4_l, h * HALF, HALF)), a_pos[t][:, cols], ALU.mult
                 )
-            if t < PACK - 1:
-                nc.vector.tensor_tensor(res[:], left[:], right[:], ALU.subtract)
-                nc.sync.dma_start(out_v[t], res[:])
-            else:
-                for h in range(2):
-                    cols = slice(h * HALF, (h + 1) * HALF)
+            width = S if t < last_t - 1 else HALF
+            for c0 in range(0, S, width):
+                cols = slice(c0, c0 + width)
+                if t < last_t:
+                    turned = psum.tile([P, width], F32, name="turned%d_%d" % (t, c0), tag="bank0")
+                    turned_sb = keep.tile([P, width], F32, name="turned_sb%d_%d" % (t, c0))
+                    back = psum.tile([P, width], F32, name="back%d_%d" % (t, c0), tag="bank%d" % PACK)
+                    for j in range(0, width, P):
+                        src = slice(c0 + j, c0 + j + P)
+                        dst = turned[:, j : j + P]
+                        nc.tensor.matmul(dst, left[:, src], ident[:], start=True, stop=False, is_transpose=True)
+                        nc.tensor.matmul(dst, right[:, src], ident[:], start=False, stop=True, is_transpose=True)
+                    nc.scalar.copy(turned_sb[:], turned[:])
+                    for j in range(0, width, P):
+                        nc.tensor.transpose(back[:, j : j + P], turned_sb[:, j : j + P], ident[:])
+                    nc.scalar.copy(res[:, cols], back[:])
+                else:
                     nc.vector.tensor_tensor(res[:, cols], left[:, cols], right[:, cols], ALU.subtract)
-                    nc.sync.dma_start(out_v[t][:, cols], res[:, cols])
+                queue = nc.scalar if t < last_t else nc.sync
+                queue.dma_start(out_v[t][:, :, cols], res[:, cols])

@@ -74,8 +74,8 @@ def tile_picked_ccmpcrossbmed_none_p_kernel(
             nc.vector.tensor_copy(picked[:], scale_table[:].indirect(lst[:]))
             dealt = keep.tile([P, S], U8, name=name + "_sc", align_bytes=64)
             nc.vector.tensor_copy(
-                dealt[:].bitcast(I32).rearrange("q (t r i) -> q t r i", t=PACK, i=4),
-                picked[:].bitcast(I32).rearrange("q (r t i) -> q t r i", t=PACK, i=4),
+                dealt[:].bitcast(I32).rearrange("q (t m) -> q t m", t=PACK),
+                picked[:].bitcast(I32).rearrange("q (m t) -> q t m", t=PACK),
             )
             pair_sc.append(dealt)
         x_w = keep.tile([P, S], U32, name="x_w", align_bytes=64)
@@ -98,7 +98,7 @@ def tile_picked_ccmpcrossbmed_none_p_kernel(
         def pick_dealt_words(name, lst, tag):
             dealt = keep.tile([P, S], U32, name=name, tag=tag, align_bytes=64)
             nc.vector.tensor_copy(
-                dealt[:].rearrange("q (t r i) -> q r t i", t=PACK, i=16), word_table[:].indirect(lst[:])
+                dealt[:].rearrange("q (t m v) -> q m t v", t=PACK, v=4), word_table[:].indirect(lst[:])
             )
             return dealt
 
@@ -201,7 +201,8 @@ def tile_picked_ccmpcrossbmed_none_p_kernel(
         nc.scalar.activation(a_win[0][:, late0:], a_late[:], COPY, scale=-OUT_SCALE)
         nc.scalar.copy(b_sb[0][:, first_w:], b_rest[:])
         nc.scalar.activation(a_pos[0][:, late0:], a_late[:], COPY, scale=OUT_SCALE)
-        for t in range(1, PACK):
+
+        def scores_out(t):
             b_bank = psum.tile([P, S], F32, name="b_bank%d" % t, tag="bank%d" % (PACK + t))
             score(b_bank[:], b_w, pair_sc[1], t, 0, S)
             a_rest = psum.tile([P, S - first_w], F32, name="a_rest%d" % t, tag="bank%d" % t)
@@ -209,7 +210,11 @@ def tile_picked_ccmpcrossbmed_none_p_kernel(
             nc.scalar.copy(b_sb[t][:], b_bank[:])
             a_out(t, a_rest[:], first_w, S)
 
-        out_v = out.rearrange("(r t i) n -> t r i n", t=PACK, i=16)
+        for t in range(1, last_t):
+            scores_out(t)
+
+        out_v = out.rearrange("(m t v) n -> t m v n", t=PACK, v=4)
+        turns = 0
         for t in range(PACK):
             left = keep.tile([P, S], F32, name="left%d" % t)
             right = keep.tile([P, S], F32, name="right%d" % t)
@@ -225,10 +230,12 @@ def tile_picked_ccmpcrossbmed_none_p_kernel(
             width = S if t < last_t - 1 else HALF
             for c0 in range(0, S, width):
                 cols = slice(c0, c0 + width)
-                if t < last_t:
-                    turned = psum.tile([P, width], F32, name="turned%d_%d" % (t, c0), tag="bank0")
+                by_tensor_engine = t < last_t - 1 or (t < last_t and c0 == 0)
+                if by_tensor_engine:
+                    turned = psum.tile([P, width], F32, name="turned%d_%d" % (t, c0), tag="bank%d" % (turns % 2))
                     turned_sb = keep.tile([P, width], F32, name="turned_sb%d_%d" % (t, c0))
-                    back = psum.tile([P, width], F32, name="back%d_%d" % (t, c0), tag="bank%d" % PACK)
+                    back = psum.tile([P, width], F32, name="back%d_%d" % (t, c0), tag="bank%d" % (PACK + turns % 2))
+                    turns = turns + 1
                     for j in range(0, width, P):
                         src = slice(c0 + j, c0 + j + P)
                         dst = turned[:, j : j + P]
@@ -239,6 +246,9 @@ def tile_picked_ccmpcrossbmed_none_p_kernel(
                         nc.tensor.transpose(back[:, j : j + P], turned_sb[:, j : j + P], ident[:])
                     nc.scalar.copy(res[:, cols], back[:])
                 else:
-                    nc.vector.tensor_tensor(res[:, cols], left[:, cols], right[:, cols], ALU.subtract)
-                queue = nc.scalar if t < last_t else nc.sync
+                    op = ALU.add if t < last_t else ALU.subtract
+                    nc.vector.tensor_tensor(res[:, cols], left[:, cols], right[:, cols], op)
+                queue = nc.scalar if by_tensor_engine else nc.sync
                 queue.dma_start(out_v[t][:, :, cols], res[:, cols])
+            if t == 0:
+                scores_out(last_t)

from contextlib import ExitStack

import concourse.mybir as mybir
from concourse.masks import make_identity

K, T, S = 512, 2048, 512
FLOPS = 3 * 2 * K * S * S

F32 = mybir.dt.float32
BF16 = mybir.dt.bfloat16
I32 = mybir.dt.int32
U32 = mybir.dt.uint32
U16 = mybir.dt.uint16
U8 = mybir.dt.uint8
FP8X4 = mybir.dt.float8_e4m3fn_x4
ALU = mybir.AluOpType
COPY = mybir.ActivationFunctionType.Copy

P = 128
PACK = 4
LIST_COLS = S // 16
CHUNKS = ((0, 256), (256, 128), (384, 128))
HALF = S // 2
OUT_SCALE = 0.75 * 0.0625 * 0.0625


def entries(offsets, start, width):
    return offsets[:, start // 16 : (start + width) // 16]


def tile_picked_ccmpcrossbmed_none_p_kernel(
    tc, x_words, x_scales, w1, gs, offs, n1, n2, ca, cb, n3, n4, out
):
    nc = tc.nc
    with ExitStack() as ctx:
        lists = ctx.enter_context(tc.tile_pool(name="lists", bufs=1))
        keep = ctx.enter_context(tc.tile_pool(name="keep", bufs=1))
        psum = ctx.enter_context(tc.psum_pool(name="psum", bufs=1))

        def load_list(name, src):
            dst = lists.tile([P, LIST_COLS], U16, name=name)
            nc.sync.dma_start(dst[:], src)
            return dst

        scale_table = keep.tile([P, T], U8, name="scale_table")
        nc.vector.memset(scale_table[:].bitcast(I32), 0)
        for q in range(4):
            nc.sync.dma_start(
                scale_table[32 * q : 32 * q + 4, :].bitcast(I32),
                x_scales[0, 4 * q : 4 * q + 4, :].bitcast(I32),
            )
        offs_l = load_list("offs_l", offs)
        ca_l = load_list("ca_l", ca)
        cb_l = load_list("cb_l", cb)
        w_raw = keep.tile([P, PACK, S], F32, name="w_raw")
        nc.sync.dma_start(w_raw[:], w1.rearrange("(p j) c -> p j c", j=PACK))
        word_table = keep.tile([P, T], U32, name="word_table")
        nc.sync.dma_start(word_table[:].bitcast(I32), x_words[0].rearrange("p c r -> p (c r)").bitcast(I32))
        gain = keep.tile([P, PACK], F32, name="gain")
        nc.sync.dma_start(gain[:], gs.rearrange("(p t) o -> p (t o)", t=PACK))
        n1_l = load_list("n1_l", n1)
        n2_l = load_list("n2_l", n2)
        n3_l = load_list("n3_l", n3)
        n4_l = load_list("n4_l", n4)
        ident = keep.tile([P, P], F32, name="ident")
        nc.vector.memset(ident[:], 0.0)
        make_identity(nc, ident[:], nomemset=True)

        x_sc = keep.tile([P, S], U8, name="x_sc", align_bytes=64)
        nc.vector.tensor_copy(x_sc[:], scale_table[:].indirect(offs_l[:]))
        pair_sc = []
        for name, lst in (("a", ca_l), ("b", cb_l)):
            picked = keep.tile([P, S], U8, name=name + "_sc_picked")
            nc.vector.tensor_copy(picked[:], scale_table[:].indirect(lst[:]))
            dealt = keep.tile([P, S], U8, name=name + "_sc", align_bytes=64)
            nc.vector.tensor_copy(
                dealt[:].bitcast(I32).rearrange("q (t m) -> q t m", t=PACK),
                picked[:].bitcast(I32).rearrange("q (m t) -> q t m", t=PACK),
            )
            pair_sc.append(dealt)
        x_w = keep.tile([P, S], U32, name="x_w", align_bytes=64)
        nc.vector.tensor_copy(x_w[:], word_table[:].indirect(offs_l[:]))

        w_q = keep.tile([P, S], U32, name="w_q", align_bytes=64)
        w_sc = keep.tile([P, S], U8, name="w_sc", align_bytes=64)
        w_raw_v = w_raw[:].rearrange("p j (m t) -> p m j t", t=PACK)
        for u in range(2):
            w_bf = keep.tile([P, 2 * S], BF16, name="w_bf%d" % u, tag="w_bf%d" % u, align_bytes=64)
            nc.scalar.activation(
                w_bf[:].rearrange("p (t m j) -> p m j t", t=2, j=PACK), w_raw_v[:, :, :, 2 * u : 2 * u + 2], COPY
            )
            nc.vector.quantize_mx(
                out=w_q[:, u * HALF : (u + 1) * HALF].bitcast(FP8X4),
                scales=w_sc[:, u * HALF : (u + 1) * HALF],
                in_=w_bf[:],
            )

        def pick_dealt_words(name, lst, tag):
            dealt = keep.tile([P, S], U32, name=name, tag=tag, align_bytes=64)
            nc.vector.tensor_copy(
                dealt[:].rearrange("q (t m v) -> q m t v", t=PACK, v=4), word_table[:].indirect(lst[:])
            )
            return dealt

        a_w = pick_dealt_words("a_w", ca_l, "w_bf1")

        y_f32 = []
        y_bank = []
        y_bf = keep.tile([P, PACK, S], BF16, name="y_bf")
        for t in range(PACK):
            bank = psum.tile([P, S], F32, name="y_bank%d" % t, tag="bank%d" % (PACK + t))
            nc.tensor.matmul_mx(
                out=bank[:],
                lhsT=w_q[:, t * P : (t + 1) * P].bitcast(FP8X4),
                lhsT_scale=w_sc[:, t * P : (t + 1) * P],
                rhs=x_w[:].bitcast(FP8X4),
                rhs_scale=x_sc[:],
                start=True,
                stop=True,
            )
            y_t = keep.tile([P, S], F32, name="y%d" % t)
            nc.scalar.activation(y_t[:], bank[:], COPY, scale=gain[:, t : t + 1])
            y_f32.append(y_t)
            y_bank.append(bank)
        for t in range(PACK):
            nc.scalar.activation(y_bf[:, t, :], y_bank[t][:], COPY, scale=gain[:, t : t + 1])

        z_q = keep.tile([P, S], U32, name="z_q", align_bytes=64)
        z_sc = keep.tile([P, S], U8, name="z_sc", align_bytes=64)

        def score(dst, words, scales, t, c0, w):
            nc.tensor.matmul_mx(
                out=dst,
                lhsT=words[:, t * P : (t + 1) * P].bitcast(FP8X4),
                lhsT_scale=scales[:, t * P : (t + 1) * P],
                rhs=z_q[:, c0 : c0 + w].bitcast(FP8X4),
                rhs_scale=z_sc[:, c0 : c0 + w],
                start=True,
                stop=True,
            )

        last_t = PACK - 1
        a_pos = [keep.tile([P, S], F32, name="a_pos%d" % t) for t in range(PACK)]
        a_win = [keep.tile([P, S], F32, name="a_neg%d" % t) for t in range(last_t)] + [a_pos[last_t]]
        b_sb = [keep.tile([P, S], F32, name="b%d" % t) for t in range(PACK)]

        def a_out(t, src, c0, c1):
            nc.scalar.activation(a_pos[t][:, c0:c1], src, COPY, scale=OUT_SCALE)
            if t < last_t:
                nc.scalar.activation(a_win[t][:, c0:c1], src, COPY, scale=-OUT_SCALE)

        last = len(CHUNKS) - 1
        late0, late_w = CHUNKS[last]
        a_early = psum.tile([P, late0], F32, name="a_early", tag="bank0")
        first_w = CHUNKS[0][1]
        for c, (c0, w) in enumerate(CHUNKS):
            pa = keep.tile([P, PACK, w], BF16, name="pa%d" % c, tag="pa")
            pb = keep.tile([P, PACK, w], BF16, name="pb%d" % c, tag="pb")
            for t in range(PACK):
                nc.vector.tensor_copy(pa[:, t, :], y_f32[t][:].indirect(entries(n1_l, c0, w)))
                if c == 0:
                    nc.vector.tensor_copy(pb[:, t, :], y_f32[t][:].indirect(entries(n2_l, c0, w)))
            if c > 0:
                for t in range(PACK):
                    nc.vector.tensor_copy(pb[:, t, :], y_f32[t][:].indirect(entries(n2_l, c0, w)))
            y_c = y_bf[:, :, c0 : c0 + w]
            hi = keep.tile([P, PACK, w], BF16, name="hi%d" % c, tag="hi%d" % c, align_bytes=64)
            lo = keep.tile([P, PACK, w], BF16, name="lo%d" % c)
            mid = keep.tile([P, PACK, w], BF16, name="mid%d" % c)
            z = keep.tile([P, PACK, w], BF16, name="z%d" % c)
            nc.vector.tensor_tensor(hi[:], y_c, pa[:], ALU.max)
            nc.vector.tensor_tensor(lo[:], y_c, pa[:], ALU.min)
            nc.vector.tensor_tensor(mid[:], hi[:], pb[:], ALU.min)
            nc.vector.tensor_tensor(z[:], lo[:], mid[:], ALU.max)
            z_k = keep.tile([P, w * PACK], BF16, name="z_k%d" % c, tag="z_k%d" % c, align_bytes=64)
            nc.scalar.copy(
                z_k[:].rearrange("p (c i t) -> p c t i", i=4, t=PACK), z[:].rearrange("p t (c i) -> p c t i", i=4)
            )
            if c == last:
                b_w = pick_dealt_words("b_w", cb_l, "hi%d" % c)
            nc.vector.quantize_mx(
                out=z_q[:, c0 : c0 + w].bitcast(FP8X4), scales=z_sc[:, c0 : c0 + w], in_=z_k[:]
            )
            if c < last:
                score(a_early[:, c0 : c0 + w], a_w, pair_sc[0], 0, c0, w)
            if c == 0:
                for t in range(1, PACK):
                    a_first = psum.tile([P, first_w], F32, name="a_first%d" % t, tag="bank%d" % t)
                    score(a_first[:], a_w, pair_sc[0], t, 0, first_w)
                    a_out(t, a_first[:], 0, first_w)
            if c == last - 1:
                a_out(0, a_early[:], 0, late0)

        b_first = psum.tile([P, first_w], F32, name="b_first", tag="bank%d" % PACK)
        score(b_first[:], b_w, pair_sc[1], 0, 0, first_w)
        a_late = psum.tile([P, late_w], F32, name="a_late", tag="bank0")
        score(a_late[:], a_w, pair_sc[0], 0, late0, late_w)
        b_rest = psum.tile([P, S - first_w], F32, name="b_rest", tag="bank%d" % (2 * PACK - 1))
        score(b_rest[:], b_w, pair_sc[1], 0, first_w, S - first_w)
        nc.scalar.copy(b_sb[0][:, :first_w], b_first[:])
        nc.scalar.activation(a_win[0][:, late0:], a_late[:], COPY, scale=-OUT_SCALE)
        nc.scalar.copy(b_sb[0][:, first_w:], b_rest[:])
        nc.scalar.activation(a_pos[0][:, late0:], a_late[:], COPY, scale=OUT_SCALE)

        def scores_out(t):
            b_bank = psum.tile([P, S], F32, name="b_bank%d" % t, tag="bank%d" % (PACK + t))
            score(b_bank[:], b_w, pair_sc[1], t, 0, S)
            a_rest = psum.tile([P, S - first_w], F32, name="a_rest%d" % t, tag="bank%d" % t)
            score(a_rest[:], a_w, pair_sc[0], t, first_w, S - first_w)
            nc.scalar.copy(b_sb[t][:], b_bank[:])
            a_out(t, a_rest[:], first_w, S)

        for t in range(1, last_t):
            scores_out(t)

        out_v = out.rearrange("(m t v) n -> t m v n", t=PACK, v=4)
        turns = 0
        for t in range(PACK):
            left = keep.tile([P, S], F32, name="left%d" % t)
            right = keep.tile([P, S], F32, name="right%d" % t)
            res = keep.tile([P, S], F32, name="res%d" % t)
            for h in range(2):
                cols = slice(h * HALF, (h + 1) * HALF)
                nc.vector.tensor_tensor(
                    right[:, cols], a_win[t][:].indirect(entries(n3_l, h * HALF, HALF)), b_sb[t][:, cols], ALU.mult
                )
                nc.vector.tensor_tensor(
                    left[:, cols], b_sb[t][:].indirect(entries(n4_l, h * HALF, HALF)), a_pos[t][:, cols], ALU.mult
                )
            width = S if t < last_t - 1 else HALF
            for c0 in range(0, S, width):
                cols = slice(c0, c0 + width)
                by_tensor_engine = t < last_t - 1 or (t < last_t and c0 == 0)
                if by_tensor_engine:
                    turned = psum.tile([P, width], F32, name="turned%d_%d" % (t, c0), tag="bank%d" % (turns % 2))
                    turned_sb = keep.tile([P, width], F32, name="turned_sb%d_%d" % (t, c0))
                    back = psum.tile([P, width], F32, name="back%d_%d" % (t, c0), tag="bank%d" % (PACK + turns % 2))
                    turns = turns + 1
                    for j in range(0, width, P):
                        src = slice(c0 + j, c0 + j + P)
                        dst = turned[:, j : j + P]
                        nc.tensor.matmul(dst, left[:, src], ident[:], start=True, stop=False, is_transpose=True)
                        nc.tensor.matmul(dst, right[:, src], ident[:], start=False, stop=True, is_transpose=True)
                    nc.scalar.copy(turned_sb[:], turned[:])
                    for j in range(0, width, P):
                        nc.tensor.transpose(back[:, j : j + P], turned_sb[:, j : j + P], ident[:])
                    nc.scalar.copy(res[:, cols], back[:])
                else:
                    op = ALU.add if t < last_t else ALU.subtract
                    nc.vector.tensor_tensor(res[:, cols], left[:, cols], right[:, cols], op)
                queue = nc.scalar if by_tensor_engine else nc.sync
                queue.dma_start(out_v[t][:, :, cols], res[:, cols])
            if t == 0:
                scores_out(last_t)
